import numpy as np
import ml_dtypes


def mxq(x, axis, fmt="e4m3"):
    dtype, down = {"e4m3": (ml_dtypes.float8_e4m3fn, 7), "e5m2": (ml_dtypes.float8_e5m2, 14)}[fmt]
    v = np.moveaxis(np.asarray(x, np.float32).astype(ml_dtypes.bfloat16).astype(np.float64), axis, -1)
    blocks = v.reshape(v.shape[:-1] + (-1, 32))
    amax = np.abs(blocks).max(-1, keepdims=True)
    byte = np.maximum(np.where(amax > 0, np.frexp(amax)[1] - 1 + 127, 0) - down, 1)
    scale = np.exp2(byte - 127.0)
    codes = (blocks / scale).astype(np.float32).astype(dtype).astype(np.float64)
    return np.moveaxis((codes * scale).reshape(v.shape), -1, axis)


WIDE = False


def mx_kscale(k):
    if not WIDE:
        return np.ones(k)
    levels = np.array([10, -10, 5, -5, 0])
    if k % 512:
        return np.exp2(np.random.permutation(np.resize(levels, k // 32))).repeat(32)
    a = np.empty((k // 512, 16))
    for p in range(k // 512):
        a[p, :8] = np.random.permutation(np.resize(levels, 8))
        for g in range(8):
            far = levels[np.abs(levels - a[p, g]) >= 10]
            a[p, g + 8] = far[np.random.randint(len(far))]
    return np.exp2(a.ravel()).repeat(32)


def f64(x):
    return np.asarray(x).astype(np.float64)


def striped(idx):
    return np.tile(idx.reshape(-1, 16).T, (8, 1)).astype(np.uint16)


def unstriped(offs):
    return offs[:16].T.reshape(-1).astype(np.int64)


def relu(v):
    return np.maximum(v, 0.0)


K, T, E, C, H, N = 1024, 512, 8, 128, 512, 128


def by_expert(wq, xq):
    return np.concatenate([wq[e].T @ xq[:, e * C:(e + 1) * C] for e in range(E)], axis=1)


def setup_inputs():
    n = np.random.standard_normal
    s = mx_kscale(K)[:, None]
    u = mx_kscale(H)
    first = np.random.permutation(np.repeat(np.arange(E), T // E))
    second = (first + 1 + np.random.permutation(np.repeat(np.arange(E - 1), -(-T // (E - 1)))[:T])) % E
    while np.bincount(second, minlength=E).max() != T // E:
        load = np.bincount(second, minlength=E); hi, lo = int(load.argmax()), int(load.argmin())
        t = np.flatnonzero((second == hi) & (first != lo))[0]; second[t] = lo
    slot_token = np.empty(E * C, np.int64); pos = np.empty((2, T), np.int64); fill = np.zeros(E, np.int64)
    place = np.stack([np.random.permutation(C) for _ in range(E)])
    for r, deal in enumerate((first, second)):
        for t in np.random.permutation(T):
            e = deal[t]; j = e * C + place[e, fill[e]]; fill[e] += 1; slot_token[j] = t; pos[r, t] = j
    g = np.random.uniform(0.2, 0.8, T)
    return {
        "xT": (n((K, T)) * s).astype(np.float32),
        "w1": (n((E, K, H)) / np.sqrt(K) / s[None] * u[None, None, :]).astype(np.float32),
        "w2": (n((E, H, N)) / np.sqrt(H) / u[None, :, None]).astype(np.float32),
        "gate": np.stack([np.tile(g, (N, 1)), np.tile(1.0 - g, (N, 1))]).astype(np.float32),
        "offs": striped(slot_token),
        "pos1": striped(pos[0]),
        "pos2": striped(pos[1]),
    }


def reference(xT, w1, w2, gate, offs, pos1, pos2):
    idx = unstriped(offs)
    xq = mxq(f64(xT)[:, idx], 0, "e4m3")
    h = relu(by_expert(mxq(f64(w1), 1, "e4m3"), xq))
    y = by_expert(mxq(f64(w2), 1, "e4m3"), mxq(h, 0, "e4m3"))
    return f64(gate[0]) * y[:, unstriped(pos1)] + f64(gate[1]) * y[:, unstriped(pos2)]

@@ -1,0 +1,229 @@
+from contextlib import ExitStack
+
+import concourse.mybir as mybir
+
+F32 = mybir.dt.float32
+BF16 = mybir.dt.bfloat16
+U32 = mybir.dt.uint32
+U16 = mybir.dt.uint16
+U8 = mybir.dt.uint8
+FP8X4 = mybir.dt.float8_e4m3fn_x4
+MULT = mybir.AluOpType.mult
+ADD = mybir.AluOpType.add
+MAX = mybir.AluOpType.max
+RELU = mybir.ActivationFunctionType.Relu
+
+P = 128
+K, T, E, C, H, N = 1024, 512, 8, 128, 512, 128
+PACK = 4
+K_PASS = P * PACK
+PASSES = K // K_PASS
+SLOTS = E * C
+FLOPS = 2 * SLOTS * (K * H + H * N)
+
+SLICES = ((0, 384), (384, 384), (768, 256))
+EXPERTS_A_SLICE = 3
+LAST_PARTS = 2
+RING = 14
+V_BLOCKS = (0, 128)
+G_BLOCKS = (0, 0)
+LAST_V_BLOCKS = (0, 128)
+X_V_BLOCKS = 80
+W2_V_COLS = 80
+W2_PIECES = ((0, 4), (4, 2), (6, 1), (7, 1))
+RELU_ON_VECTOR = ()
+
+
+def shared_copy(nc, dst, src, v_count, g_count=0):
+    total = dst.shape[1]
+    if v_count > 0:
+        nc.vector.tensor_copy(out=dst[:, 0:v_count], in_=src[:, 0:v_count])
+    if g_count > 0:
+        nc.gpsimd.tensor_scalar(
+            out=dst[:, v_count : v_count + g_count].rearrange("p m j t -> p t m j"),
+            in0=src[:, v_count : v_count + g_count].rearrange("p m j t -> p t m j"),
+            scalar1=1.0,
+            scalar2=0.0,
+            op0=MULT,
+            op1=ADD,
+        )
+    if v_count + g_count < total:
+        nc.scalar.copy(out=dst[:, v_count + g_count : total], in_=src[:, v_count + g_count : total])
+
+
+def tile_routed_moe_kernel(tc, xT, w1, w2, gate, offs, pos1, pos2, out):
+    nc = tc.nc
+    with ExitStack() as ctx:
+        lists = ctx.enter_context(tc.tile_pool(name="lists", bufs=1))
+        keep = ctx.enter_context(tc.tile_pool(name="keep", bufs=1))
+        ring = ctx.enter_context(tc.tile_pool(name="ring", bufs=RING))
+        stage = ctx.enter_context(tc.tile_pool(name="stage", bufs=5))
+        wq = ctx.enter_context(tc.tile_pool(name="wq", bufs=4))
+        gat = ctx.enter_context(tc.tile_pool(name="gat", bufs=2))
+        hst = ctx.enter_context(tc.tile_pool(name="hst", bufs=2))
+        psum_h = ctx.enter_context(tc.psum_pool(name="psum_h", bufs=3))
+        psum_y = ctx.enter_context(tc.psum_pool(name="psum_y", bufs=1))
+
+        offs_t = lists.tile([P, SLOTS // 16], U16, name="offs_t")
+        nc.sync.dma_start(offs_t[:], offs)
+        x_raw = []
+        for s in range(PASSES):
+            r = ring.tile([P, PACK, T], F32, name="x_raw", tag="raw")
+            nc.sync.dma_start(out=r[:], in_=xT[s * K_PASS : (s + 1) * K_PASS, :].rearrange("(p j) t -> p j t", j=PACK))
+            x_raw.append(r)
+        pos1_t = lists.tile([P, T // 16], U16, name="pos1_t")
+        nc.sync.dma_start(pos1_t[:], pos1)
+        pos2_t = lists.tile([P, T // 16], U16, name="pos2_t")
+        nc.sync.dma_start(pos2_t[:], pos2)
+        w1_raw = []
+        for e in range(E):
+            for s in range(PASSES):
+                rows = w1[e, s * K_PASS : (s + 1) * K_PASS, :].rearrange("(p j) c -> p j c", j=PACK)
+                parts = LAST_PARTS if (e == E - 1 and s == PASSES - 1) else 1
+                width = H // parts
+                pieces = []
+                for a in range(parts):
+                    r = ring.tile([P, PACK, width], F32, name="w1_raw", tag="raw")
+                    nc.sync.dma_start(out=r[:], in_=rows[:, :, a * width : (a + 1) * width])
+                    pieces.append(r)
+                w1_raw.append(pieces)
+        w2_raw = []
+        for e0, g in W2_PIECES:
+            r = ring.tile([P, g, PACK, N], F32, name="w2_raw", tag="raw")
+            nc.sync.dma_start(out=r[:], in_=w2[e0 : e0 + g].rearrange("e (p j) n -> p e j n", j=PACK))
+            w2_raw.append(r)
+        gate_t = ring.tile([P, 2, T], F32, name="gate_t", tag="raw")
+        nc.sync.dma_start(out=gate_t[:], in_=gate.rearrange("r n t -> n r t"))
+
+        x_words = []
+        for s in range(PASSES):
+            xw = keep.tile([P, T], U32, name="x_words%d" % s, align_bytes=64)
+            x_words.append(xw)
+        x_bytes = keep.tile([P, T], U8, name="x_bytes", align_bytes=64)
+        nc.gpsimd.memset(x_bytes[:], 0)
+        x_planes = [x_bytes[PACK * s : P, :] for s in range(PASSES)]
+
+        x_st = []
+        for s in range(PASSES):
+            st = stage.tile([P, PACK * T], BF16, name="x_st", tag="xst", align_bytes=64, bufs=2)
+            shared_copy(
+                nc,
+                st[:].rearrange("p (c i j) -> p c j i", i=4, j=PACK),
+                x_raw[s][:].rearrange("p j (c i) -> p c j i", i=4),
+                X_V_BLOCKS if s == 0 else 0,
+            )
+            x_st.append(st)
+        for s in range(PASSES):
+            nc.vector.quantize_mx(out=x_words[s][:].bitcast(FP8X4), scales=x_planes[s], in_=x_st[s][:])
+
+        def gather(q):
+            j0, n = SLICES[q]
+            picks = offs_t[:, j0 // 16 : (j0 + n) // 16]
+            gw = gat.tile([P, PASSES, n], U32, name="g_words", tag="gw", align_bytes=64)
+            for s in range(PASSES):
+                nc.vector.tensor_copy(out=gw[:, s, :], in_=x_words[s][:].indirect(picks))
+            gb = gat.tile([P, n], U8, name="g_bytes", tag="gb", align_bytes=64)
+            nc.vector.tensor_copy(out=gb[:], in_=x_bytes[:].indirect(picks))
+            return gw, gb
+
+        h_words = keep.tile([P, SLOTS], U32, name="h_words", align_bytes=64)
+        h_bytes = keep.tile([P, SLOTS], U8, name="h_bytes", align_bytes=64)
+        for e in range(E):
+            last = e == E - 1
+            st = stage.tile([P, PASSES * PACK * H], BF16, name="w1_st", tag="st", align_bytes=64)
+            wc = wq.tile([P, PASSES * H], U32, name="w1_words", tag="wc", align_bytes=64)
+            ws = wq.tile([P, PASSES * H], U8, name="w1_bytes", tag="ws", align_bytes=64)
+            for s in range(PASSES):
+                pieces = w1_raw[e * PASSES + s]
+                blocks = P // len(pieces)
+                whole = st[:, s * PACK * H : (s + 1) * PACK * H].rearrange("p (t m j) -> p m j t", t=4, j=PACK)
+                for a, r in enumerate(pieces):
+                    shared_copy(
+                        nc,
+                        whole[:, a * blocks : (a + 1) * blocks],
+                        r[:].rearrange("p j (m t) -> p m j t", t=4),
+                        blocks if s == 1 else 0,
+                    )
+                if last:
+                    nc.vector.quantize_mx(
+                        out=wc[:, s * H : (s + 1) * H].bitcast(FP8X4),
+                        scales=ws[:, s * H : (s + 1) * H],
+                        in_=st[:, s * PACK * H : (s + 1) * PACK * H],
+                    )
+            if not last:
+                nc.vector.quantize_mx(out=wc[:].bitcast(FP8X4), scales=ws[:], in_=st[:])
+            if e % EXPERTS_A_SLICE == 0:
+                g_words, g_bytes = gather(e // EXPERTS_A_SLICE)
+            mine = slice((e % EXPERTS_A_SLICE) * C, (e % EXPERTS_A_SLICE + 1) * C)
+            ph = psum_h.tile([P, 4, C], F32, name="ph", tag="ph")
+            for t in range(4):
+                for s in range(PASSES):
+                    w_cols = slice(s * H + t * P, s * H + (t + 1) * P)
+                    nc.tensor.matmul_mx(
+                        out=ph[:, t, :],
+                        lhsT=wc[:, w_cols].bitcast(FP8X4),
+                        lhsT_scale=ws[:, w_cols],
+                        rhs=g_words[:, s, mine].bitcast(FP8X4),
+                        rhs_scale=g_bytes[PACK * s : P, mine],
+                        start=(s == 0),
+                        stop=(s == PASSES - 1),
+                    )
+            if e % 2 == 0:
+                hb = hst.tile([P, 2 * PACK * C], BF16, name="hb", tag="hb", align_bytes=64)
+            half = hb[:, (e % 2) * PACK * C : (e % 2 + 1) * PACK * C].rearrange("p (n t) -> p n t", t=4)
+            if e in RELU_ON_VECTOR:
+                nc.vector.tensor_scalar_max(out=half, in0=ph[:].rearrange("p t n -> p n t"), scalar1=0.0)
+            else:
+                nc.scalar.activation(out=half, in_=ph[:].rearrange("p t n -> p n t"), func=RELU)
+            if e >= E - 2:
+                one_e = slice(e * C, (e + 1) * C)
+                nc.vector.quantize_mx(
+                    out=h_words[:, one_e].bitcast(FP8X4),
+                    scales=h_bytes[:, one_e],
+                    in_=hb[:, (e % 2) * PACK * C : (e % 2 + 1) * PACK * C],
+                )
+            elif e % 2 == 1:
+                pair = slice((e - 1) * C, (e + 1) * C)
+                nc.vector.quantize_mx(out=h_words[:, pair].bitcast(FP8X4), scales=h_bytes[:, pair], in_=hb[:])
+
+        w2_words = keep.tile([P, E * N], U32, name="w2_words", align_bytes=64)
+        w2_bytes = keep.tile([P, E * N], U8, name="w2_bytes", align_bytes=64)
+        y_sb = keep.tile([P, SLOTS], F32, name="y_sb")
+        for i, (e0, g) in enumerate(W2_PIECES):
+            st = stage.tile([P, g * PACK * N], BF16, name="w2_st", tag="w2st", align_bytes=64, bufs=2)
+            dst = st[:].rearrange("p (e n j) -> p e n j", e=g, j=PACK)
+            src = w2_raw[i][:].rearrange("p e j n -> p e n j")
+            if g > 1:
+                v_e = (3 * g) // 4
+                nc.vector.tensor_copy(out=dst[:, 0:v_e], in_=src[:, 0:v_e])
+                nc.scalar.copy(out=dst[:, v_e:g], in_=src[:, v_e:g])
+            else:
+                nc.vector.tensor_copy(out=dst[:, :, 0:W2_V_COLS, :], in_=src[:, :, 0:W2_V_COLS, :])
+                nc.scalar.copy(out=dst[:, :, W2_V_COLS:N, :], in_=src[:, :, W2_V_COLS:N, :])
+            cols = slice(e0 * N, (e0 + g) * N)
+            nc.vector.quantize_mx(out=w2_words[:, cols].bitcast(FP8X4), scales=w2_bytes[:, cols], in_=st[:])
+            py = psum_y.tile([P, g, C], F32, name="py%d" % i)
+            for a in range(g):
+                one = slice((e0 + a) * C, (e0 + a + 1) * C)
+                nc.tensor.matmul_mx(
+                    out=py[:, a, :],
+                    lhsT=w2_words[:, one].bitcast(FP8X4),
+                    lhsT_scale=w2_bytes[:, one],
+                    rhs=h_words[:, one].bitcast(FP8X4),
+                    rhs_scale=h_bytes[:, one],
+                    start=True,
+                    stop=True,
+                )
+            y_cols = y_sb[:, e0 * C : (e0 + g) * C]
+            if i < len(W2_PIECES) - 1:
+                nc.scalar.copy(out=y_cols, in_=py[:].rearrange("p a c -> p (a c)"))
+            else:
+                nc.vector.tensor_copy(out=y_cols, in_=py[:].rearrange("p a c -> p (a c)"))
+
+        first = keep.tile([P, T], F32, name="first")
+        second = keep.tile([P, T], F32, name="second")
+        total = keep.tile([P, T], F32, name="total")
+        nc.vector.tensor_tensor(first[:], y_sb[:].indirect(pos1_t[:]), gate_t[:, 0, :], MULT)
+        nc.vector.tensor_tensor(second[:], y_sb[:].indirect(pos2_t[:]), gate_t[:, 1, :], MULT)
+        nc.vector.tensor_tensor(total[:], first[:], second[:], ADD)
+        nc.sync.dma_start(out=out, in_=total[:])

@@ -31,6 +31,7 @@ LAST_V_BLOCKS = (0, 128)
 X_V_BLOCKS = 80
 W2_V_COLS = 80
 W2_PIECES = ((0, 4), (4, 2), (6, 1), (7, 1))
+W2_EARLY = 1
 RELU_ON_VECTOR = ()
 
 
@@ -75,6 +76,15 @@ def tile_routed_moe_kernel(tc, xT, w1, w2, gate, offs, pos1, pos2, out):
         nc.sync.dma_start(pos1_t[:], pos1)
         pos2_t = lists.tile([P, T // 16], U16, name="pos2_t")
         nc.sync.dma_start(pos2_t[:], pos2)
+        w2_raw = []
+
+        def load_w2(e0, g):
+            r = ring.tile([P, g, PACK, N], F32, name="w2_raw", tag="raw")
+            nc.sync.dma_start(out=r[:], in_=w2[e0 : e0 + g].rearrange("e (p j) n -> p e j n", j=PACK))
+            w2_raw.append(r)
+
+        for e0, g in W2_PIECES[:W2_EARLY]:
+            load_w2(e0, g)
         w1_raw = []
         for e in range(E):
             for s in range(PASSES):
@@ -87,11 +97,8 @@ def tile_routed_moe_kernel(tc, xT, w1, w2, gate, offs, pos1, pos2, out):
                     nc.sync.dma_start(out=r[:], in_=rows[:, :, a * width : (a + 1) * width])
                     pieces.append(r)
                 w1_raw.append(pieces)
-        w2_raw = []
-        for e0, g in W2_PIECES:
-            r = ring.tile([P, g, PACK, N], F32, name="w2_raw", tag="raw")
-            nc.sync.dma_start(out=r[:], in_=w2[e0 : e0 + g].rearrange("e (p j) n -> p e j n", j=PACK))
-            w2_raw.append(r)
+        for e0, g in W2_PIECES[W2_EARLY:]:
+            load_w2(e0, g)
         gate_t = ring.tile([P, 2, T], F32, name="gate_t", tag="raw")
         nc.sync.dma_start(out=gate_t[:], in_=gate.rearrange("r n t -> n r t"))
 
@@ -128,6 +135,52 @@ def tile_routed_moe_kernel(tc, xT, w1, w2, gate, offs, pos1, pos2, out):
 
         h_words = keep.tile([P, SLOTS], U32, name="h_words", align_bytes=64)
         h_bytes = keep.tile([P, SLOTS], U8, name="h_bytes", align_bytes=64)
+        w2_words = keep.tile([P, E * N], U32, name="w2_words", align_bytes=64)
+        w2_bytes = keep.tile([P, E * N], U8, name="w2_bytes", align_bytes=64)
+        y_sb = keep.tile([P, SLOTS], F32, name="y_sb")
+        py_of = {}
+
+        def quantise_w2(i):
+            e0, g = W2_PIECES[i]
+            st = stage.tile([P, g * PACK * N], BF16, name="w2_st", tag="w2st", align_bytes=64, bufs=2)
+            dst = st[:].rearrange("p (e n j) -> p e n j", e=g, j=PACK)
+            src = w2_raw[i][:].rearrange("p e j n -> p e n j")
+            if i < W2_EARLY:
+                for a in range(0, g, 2):
+                    nc.scalar.copy(out=dst[:, a : a + 2], in_=src[:, a : a + 2])
+            elif g > 1:
+                v_e = g // 2
+                nc.vector.tensor_copy(out=dst[:, 0:v_e], in_=src[:, 0:v_e])
+                nc.scalar.copy(out=dst[:, v_e:g], in_=src[:, v_e:g])
+            else:
+                nc.vector.tensor_copy(out=dst[:, :, 0:W2_V_COLS, :], in_=src[:, :, 0:W2_V_COLS, :])
+                nc.scalar.copy(out=dst[:, :, W2_V_COLS:N, :], in_=src[:, :, W2_V_COLS:N, :])
+            cols = slice(e0 * N, (e0 + g) * N)
+            nc.vector.quantize_mx(out=w2_words[:, cols].bitcast(FP8X4), scales=w2_bytes[:, cols], in_=st[:])
+            py = psum_y.tile([P, g, C], F32, name="py%d" % i)
+            for a in range(g):
+                py_of[e0 + a] = (py, a)
+
+        def layer2(e0, g, on_vector):
+            py, a0 = py_of[e0]
+            for a in range(g):
+                one = slice((e0 + a) * C, (e0 + a + 1) * C)
+                nc.tensor.matmul_mx(
+                    out=py[:, a0 + a, :],
+                    lhsT=w2_words[:, one].bitcast(FP8X4),
+                    lhsT_scale=w2_bytes[:, one],
+                    rhs=h_words[:, one].bitcast(FP8X4),
+                    rhs_scale=h_bytes[:, one],
+                    start=True,
+                    stop=True,
+                )
+            y_cols = y_sb[:, e0 * C : (e0 + g) * C]
+            if on_vector:
+                nc.vector.tensor_copy(out=y_cols, in_=py[:, a0 : a0 + g, :].rearrange("p a c -> p (a c)"))
+            else:
+                nc.scalar.copy(out=y_cols, in_=py[:, a0 : a0 + g, :].rearrange("p a c -> p (a c)"))
+
+        early_experts = sum(g for e0, g in W2_PIECES[:W2_EARLY])
         for e in range(E):
             last = e == E - 1
             st = stage.tile([P, PASSES * PACK * H], BF16, name="w1_st", tag="st", align_bytes=64)
@@ -185,40 +238,15 @@ def tile_routed_moe_kernel(tc, xT, w1, w2, gate, offs, pos1, pos2, out):
             elif e % 2 == 1:
                 pair = slice((e - 1) * C, (e + 1) * C)
                 nc.vector.quantize_mx(out=h_words[:, pair].bitcast(FP8X4), scales=h_bytes[:, pair], in_=hb[:])
+                if e == 1:
+                    for i in range(W2_EARLY):
+                        quantise_w2(i)
+                if e < early_experts:
+                    layer2(e - 1, 2, False)
 
-        w2_words = keep.tile([P, E * N], U32, name="w2_words", align_bytes=64)
-        w2_bytes = keep.tile([P, E * N], U8, name="w2_bytes", align_bytes=64)
-        y_sb = keep.tile([P, SLOTS], F32, name="y_sb")
-        for i, (e0, g) in enumerate(W2_PIECES):
-            st = stage.tile([P, g * PACK * N], BF16, name="w2_st", tag="w2st", align_bytes=64, bufs=2)
-            dst = st[:].rearrange("p (e n j) -> p e n j", e=g, j=PACK)
-            src = w2_raw[i][:].rearrange("p e j n -> p e n j")
-            if g > 1:
-                v_e = (3 * g) // 4
-                nc.vector.tensor_copy(out=dst[:, 0:v_e], in_=src[:, 0:v_e])
-                nc.scalar.copy(out=dst[:, v_e:g], in_=src[:, v_e:g])
-            else:
-                nc.vector.tensor_copy(out=dst[:, :, 0:W2_V_COLS, :], in_=src[:, :, 0:W2_V_COLS, :])
-                nc.scalar.copy(out=dst[:, :, W2_V_COLS:N, :], in_=src[:, :, W2_V_COLS:N, :])
-            cols = slice(e0 * N, (e0 + g) * N)
-            nc.vector.quantize_mx(out=w2_words[:, cols].bitcast(FP8X4), scales=w2_bytes[:, cols], in_=st[:])
-            py = psum_y.tile([P, g, C], F32, name="py%d" % i)
-            for a in range(g):
-                one = slice((e0 + a) * C, (e0 + a + 1) * C)
-                nc.tensor.matmul_mx(
-                    out=py[:, a, :],
-                    lhsT=w2_words[:, one].bitcast(FP8X4),
-                    lhsT_scale=w2_bytes[:, one],
-                    rhs=h_words[:, one].bitcast(FP8X4),
-                    rhs_scale=h_bytes[:, one],
-                    start=True,
-                    stop=True,
-                )
-            y_cols = y_sb[:, e0 * C : (e0 + g) * C]
-            if i < len(W2_PIECES) - 1:
-                nc.scalar.copy(out=y_cols, in_=py[:].rearrange("p a c -> p (a c)"))
-            else:
-                nc.vector.tensor_copy(out=y_cols, in_=py[:].rearrange("p a c -> p (a c)"))
+        for i in range(W2_EARLY, len(W2_PIECES)):
+            quantise_w2(i)
+            layer2(W2_PIECES[i][0], W2_PIECES[i][1], i == len(W2_PIECES) - 1)
 
         first = keep.tile([P, T], F32, name="first")
         second = keep.tile([P, T], F32, name="second")

@@ -208,26 +208,41 @@ def tile_routed_moe_kernel(tc, xT, w1, w2, gate, offs, pos1, pos2, out):
             if e % EXPERTS_A_SLICE == 0:
                 g_words, g_bytes = gather(e // EXPERTS_A_SLICE)
             mine = slice((e % EXPERTS_A_SLICE) * C, (e % EXPERTS_A_SLICE + 1) * C)
-            ph = psum_h.tile([P, 4, C], F32, name="ph", tag="ph")
-            for t in range(4):
-                for s in range(PASSES):
-                    w_cols = slice(s * H + t * P, s * H + (t + 1) * P)
-                    nc.tensor.matmul_mx(
-                        out=ph[:, t, :],
-                        lhsT=wc[:, w_cols].bitcast(FP8X4),
-                        lhsT_scale=ws[:, w_cols],
-                        rhs=g_words[:, s, mine].bitcast(FP8X4),
-                        rhs_scale=g_bytes[PACK * s : P, mine],
-                        start=(s == 0),
-                        stop=(s == PASSES - 1),
-                    )
+            banks = 2 if last else 1
+            t_a_bank = 4 // banks
+            phs = []
+            for b in range(banks):
+                ph = psum_h.tile([P, t_a_bank, C], F32, name="ph", tag="ph")
+                phs.append(ph)
+
+            def pass_of(t, s):
+                w_cols = slice(s * H + t * P, s * H + (t + 1) * P)
+                nc.tensor.matmul_mx(
+                    out=phs[t // t_a_bank][:, t % t_a_bank, :],
+                    lhsT=wc[:, w_cols].bitcast(FP8X4),
+                    lhsT_scale=ws[:, w_cols],
+                    rhs=g_words[:, s, mine].bitcast(FP8X4),
+                    rhs_scale=g_bytes[PACK * s : P, mine],
+                    start=(s == 0),
+                    stop=(s == PASSES - 1),
+                )
+
+            for b in range(banks):
+                pass_of(b * t_a_bank, 0)
+            for b in range(banks):
+                pass_of(b * t_a_bank, 1)
+                for t in range(b * t_a_bank + 1, (b + 1) * t_a_bank):
+                    for s in range(PASSES):
+                        pass_of(t, s)
             if e % 2 == 0:
                 hb = hst.tile([P, 2 * PACK * C], BF16, name="hb", tag="hb", align_bytes=64)
             half = hb[:, (e % 2) * PACK * C : (e % 2 + 1) * PACK * C].rearrange("p (n t) -> p n t", t=4)
-            if e in RELU_ON_VECTOR:
-                nc.vector.tensor_scalar_max(out=half, in0=ph[:].rearrange("p t n -> p n t"), scalar1=0.0)
-            else:
-                nc.scalar.activation(out=half, in_=ph[:].rearrange("p t n -> p n t"), func=RELU)
+            for b in range(banks):
+                part = half[:, :, b * t_a_bank : (b + 1) * t_a_bank]
+                if b == 1:
+                    nc.vector.tensor_scalar_max(out=part, in0=phs[b][:].rearrange("p t n -> p n t"), scalar1=0.0)
+                else:
+                    nc.scalar.activation(out=part, in_=phs[b][:].rearrange("p t n -> p n t"), func=RELU)
             if e >= E - 2:
                 one_e = slice(e * C, (e + 1) * C)
                 nc.vector.quantize_mx(

@@ -23,7 +23,7 @@ FLOPS = 2 * SLOTS * (K * H + H * N)
 
 SLICES = ((0, 384), (384, 384), (768, 256))
 EXPERTS_A_SLICE = 3
-LAST_PARTS = 2
+LAST_WIDTHS = (256, 128, 128)
 RING = 14
 V_BLOCKS = (0, 128)
 G_BLOCKS = (0, 0)
@@ -89,13 +89,14 @@ def tile_routed_moe_kernel(tc, xT, w1, w2, gate, offs, pos1, pos2, out):
         for e in range(E):
             for s in range(PASSES):
                 rows = w1[e, s * K_PASS : (s + 1) * K_PASS, :].rearrange("(p j) c -> p j c", j=PACK)
-                parts = LAST_PARTS if (e == E - 1 and s == PASSES - 1) else 1
-                width = H // parts
+                widths = LAST_WIDTHS if (e == E - 1 and s == PASSES - 1) else (H,)
                 pieces = []
-                for a in range(parts):
+                c0 = 0
+                for width in widths:
                     r = ring.tile([P, PACK, width], F32, name="w1_raw", tag="raw")
-                    nc.sync.dma_start(out=r[:], in_=rows[:, :, a * width : (a + 1) * width])
-                    pieces.append(r)
+                    nc.sync.dma_start(out=r[:], in_=rows[:, :, c0 : c0 + width])
+                    pieces.append((r, c0 // 4, width // 4))
+                    c0 += width
                 w1_raw.append(pieces)
         for e0, g in W2_PIECES[W2_EARLY:]:
             load_w2(e0, g)
@@ -188,12 +189,11 @@ def tile_routed_moe_kernel(tc, xT, w1, w2, gate, offs, pos1, pos2, out):
             ws = wq.tile([P, PASSES * H], U8, name="w1_bytes", tag="ws", align_bytes=64)
             for s in range(PASSES):
                 pieces = w1_raw[e * PASSES + s]
-                blocks = P // len(pieces)
                 whole = st[:, s * PACK * H : (s + 1) * PACK * H].rearrange("p (t m j) -> p m j t", t=4, j=PACK)
-                for a, r in enumerate(pieces):
+                for r, m0, blocks in pieces:
                     shared_copy(
                         nc,
-                        whole[:, a * blocks : (a + 1) * blocks],
+                        whole[:, m0 : m0 + blocks],
                         r[:].rearrange("p j (m t) -> p m j t", t=4),
                         blocks if s == 1 else 0,
                     )

@@ -24,15 +24,15 @@ FLOPS = 2 * SLOTS * (K * H + H * N)
 SLICES = ((0, 384), (384, 384), (768, 256))
 EXPERTS_A_SLICE = 3
 LAST_WIDTHS = (256, 128, 128)
-RING = 14
+RING = 13
 V_BLOCKS = (0, 128)
 G_BLOCKS = (0, 0)
 LAST_V_BLOCKS = (0, 128)
 X_V_BLOCKS = 80
-W2_V_COLS = 80
 W2_PIECES = ((0, 4), (4, 2), (6, 1), (7, 1))
+LATE_LAYER2 = ((4, 3), (7, 1))
 W2_EARLY = 1
-RELU_ON_VECTOR = ()
+TOKEN_CUTS = (320, 192)
 
 
 def shared_copy(nc, dst, src, v_count, g_count=0):
@@ -62,7 +62,8 @@ def tile_routed_moe_kernel(tc, xT, w1, w2, gate, offs, pos1, pos2, out):
         wq = ctx.enter_context(tc.tile_pool(name="wq", bufs=4))
         gat = ctx.enter_context(tc.tile_pool(name="gat", bufs=2))
         hst = ctx.enter_context(tc.tile_pool(name="hst", bufs=2))
-        psum_h = ctx.enter_context(tc.psum_pool(name="psum_h", bufs=3))
+        late = ctx.enter_context(tc.tile_pool(name="late", bufs=1))
+        psum_h = ctx.enter_context(tc.psum_pool(name="psum_h", bufs=2))
         psum_y = ctx.enter_context(tc.psum_pool(name="psum_y", bufs=1))
 
         offs_t = lists.tile([P, SLOTS // 16], U16, name="offs_t")
@@ -79,7 +80,10 @@ def tile_routed_moe_kernel(tc, xT, w1, w2, gate, offs, pos1, pos2, out):
         w2_raw = []
 
         def load_w2(e0, g):
-            r = ring.tile([P, g, PACK, N], F32, name="w2_raw", tag="raw")
+            if e0 + g == E:
+                r = late.tile([P, g, PACK, N], F32, name="w2_last", tag="late", align_bytes=64)
+            else:
+                r = ring.tile([P, g, PACK, N], F32, name="w2_raw", tag="raw")
             nc.sync.dma_start(out=r[:], in_=w2[e0 : e0 + g].rearrange("e (p j) n -> p e j n", j=PACK))
             w2_raw.append(r)
 
@@ -93,7 +97,10 @@ def tile_routed_moe_kernel(tc, xT, w1, w2, gate, offs, pos1, pos2, out):
                 pieces = []
                 c0 = 0
                 for width in widths:
-                    r = ring.tile([P, PACK, width], F32, name="w1_raw", tag="raw")
+                    if e == E - 1 and s == PASSES - 1 and c0 + width == H:
+                        r = late.tile([P, PACK, width], F32, name="w1_last", tag="late_w1", align_bytes=64)
+                    else:
+                        r = ring.tile([P, PACK, width], F32, name="w1_raw", tag="raw")
                     nc.sync.dma_start(out=r[:], in_=rows[:, :, c0 : c0 + width])
                     pieces.append((r, c0 // 4, width // 4))
                     c0 += width
@@ -138,12 +145,12 @@ def tile_routed_moe_kernel(tc, xT, w1, w2, gate, offs, pos1, pos2, out):
         h_bytes = keep.tile([P, SLOTS], U8, name="h_bytes", align_bytes=64)
         w2_words = keep.tile([P, E * N], U32, name="w2_words", align_bytes=64)
         w2_bytes = keep.tile([P, E * N], U8, name="w2_bytes", align_bytes=64)
+        h_scales = [h_bytes[:, e * C : (e + 1) * C] for e in range(E)]
         y_sb = keep.tile([P, SLOTS], F32, name="y_sb")
-        py_of = {}
 
         def quantise_w2(i):
             e0, g = W2_PIECES[i]
-            st = stage.tile([P, g * PACK * N], BF16, name="w2_st", tag="w2st", align_bytes=64, bufs=2)
+            st = stage.tile([P, g * PACK * N], BF16, name="w2_st", tag="w2st", align_bytes=64, bufs=4)
             dst = st[:].rearrange("p (e n j) -> p e n j", e=g, j=PACK)
             src = w2_raw[i][:].rearrange("p e j n -> p e n j")
             if i < W2_EARLY:
@@ -153,43 +160,56 @@ def tile_routed_moe_kernel(tc, xT, w1, w2, gate, offs, pos1, pos2, out):
                 v_e = g // 2
                 nc.vector.tensor_copy(out=dst[:, 0:v_e], in_=src[:, 0:v_e])
                 nc.scalar.copy(out=dst[:, v_e:g], in_=src[:, v_e:g])
+            elif i % 2 == 0:
+                nc.vector.tensor_copy(out=dst, in_=src)
             else:
-                nc.vector.tensor_copy(out=dst[:, :, 0:W2_V_COLS, :], in_=src[:, :, 0:W2_V_COLS, :])
-                nc.scalar.copy(out=dst[:, :, W2_V_COLS:N, :], in_=src[:, :, W2_V_COLS:N, :])
+                nc.scalar.copy(out=dst, in_=src)
             cols = slice(e0 * N, (e0 + g) * N)
             nc.vector.quantize_mx(out=w2_words[:, cols].bitcast(FP8X4), scales=w2_bytes[:, cols], in_=st[:])
-            py = psum_y.tile([P, g, C], F32, name="py%d" % i)
-            for a in range(g):
-                py_of[e0 + a] = (py, a)
 
-        def layer2(e0, g, on_vector):
-            py, a0 = py_of[e0]
+        def layer2(e0, g):
+            if e0 == LATE_LAYER2[0][0]:
+                py = psum_h.tile([P, g, C], F32, name="py_late", tag="ph")
+            else:
+                py = psum_y.tile([P, g, C], F32, name="py%d" % e0)
             for a in range(g):
                 one = slice((e0 + a) * C, (e0 + a + 1) * C)
                 nc.tensor.matmul_mx(
-                    out=py[:, a0 + a, :],
+                    out=py[:, a, :],
                     lhsT=w2_words[:, one].bitcast(FP8X4),
                     lhsT_scale=w2_bytes[:, one],
                     rhs=h_words[:, one].bitcast(FP8X4),
-                    rhs_scale=h_bytes[:, one],
+                    rhs_scale=h_scales[e0 + a],
                     start=True,
                     stop=True,
                 )
             y_cols = y_sb[:, e0 * C : (e0 + g) * C]
-            if on_vector:
-                nc.vector.tensor_copy(out=y_cols, in_=py[:, a0 : a0 + g, :].rearrange("p a c -> p (a c)"))
-            else:
-                nc.scalar.copy(out=y_cols, in_=py[:, a0 : a0 + g, :].rearrange("p a c -> p (a c)"))
+            nc.scalar.copy(out=y_cols, in_=py[:].rearrange("p a c -> p (a c)"))
+
+        def quantise_h(e, hb, scales):
+            one = slice(e * C, (e + 1) * C)
+            nc.vector.quantize_mx(out=h_words[:, one].bitcast(FP8X4), scales=scales, in_=hb[:, 0 : PACK * C])
+            h_scales[e] = scales
 
         early_experts = sum(g for e0, g in W2_PIECES[:W2_EARLY])
         for e in range(E):
             last = e == E - 1
-            st = stage.tile([P, PASSES * PACK * H], BF16, name="w1_st", tag="st", align_bytes=64)
+            if last:
+                st_of = [
+                    stage.tile([P, PACK * H], BF16, name="w1_st_last", tag="st", align_bytes=64),
+                    late.tile([P, PACK * H], BF16, name="w1_st_late", tag="late_st", align_bytes=64),
+                ]
+            else:
+                st = stage.tile([P, PASSES * PACK * H], BF16, name="w1_st", tag="st", align_bytes=64)
+                st_of = [st[:, s * PACK * H : (s + 1) * PACK * H] for s in range(PASSES)]
             wc = wq.tile([P, PASSES * H], U32, name="w1_words", tag="wc", align_bytes=64)
-            ws = wq.tile([P, PASSES * H], U8, name="w1_bytes", tag="ws", align_bytes=64)
+            if last:
+                ws = late.tile([P, PASSES * H], U8, name="w1_bytes_last", tag="late_w1", align_bytes=64)
+            else:
+                ws = wq.tile([P, PASSES * H], U8, name="w1_bytes", tag="ws", align_bytes=64)
             for s in range(PASSES):
                 pieces = w1_raw[e * PASSES + s]
-                whole = st[:, s * PACK * H : (s + 1) * PACK * H].rearrange("p (t m j) -> p m j t", t=4, j=PACK)
+                whole = st_of[s][:, 0 : PACK * H].rearrange("p (t m j) -> p m j t", t=4, j=PACK)
                 for r, m0, blocks in pieces:
                     shared_copy(
                         nc,
@@ -201,9 +221,12 @@ def tile_routed_moe_kernel(tc, xT, w1, w2, gate, offs, pos1, pos2, out):
                     nc.vector.quantize_mx(
                         out=wc[:, s * H : (s + 1) * H].bitcast(FP8X4),
                         scales=ws[:, s * H : (s + 1) * H],
-                        in_=st[:, s * PACK * H : (s + 1) * PACK * H],
+                        in_=st_of[s][:, 0 : PACK * H],
                     )
-            if not last:
+            if last:
+                before_scales = late.tile([P, C], U8, name="h_bytes_before", tag="late_st", align_bytes=64)
+                quantise_h(E - 2, hb_before, before_scales[:])
+            else:
                 nc.vector.quantize_mx(out=wc[:].bitcast(FP8X4), scales=ws[:], in_=st[:])
             if e % EXPERTS_A_SLICE == 0:
                 g_words, g_bytes = gather(e // EXPERTS_A_SLICE)
@@ -234,22 +257,19 @@ def tile_routed_moe_kernel(tc, xT, w1, w2, gate, offs, pos1, pos2, out):
                 for t in range(b * t_a_bank + 1, (b + 1) * t_a_bank):
                     for s in range(PASSES):
                         pass_of(t, s)
-            if e % 2 == 0:
+            if last:
+                hb = late.tile([P, PACK * C], BF16, name="hb_last", tag="late", align_bytes=64)
+            elif e % 2 == 0:
                 hb = hst.tile([P, 2 * PACK * C], BF16, name="hb", tag="hb", align_bytes=64)
-            half = hb[:, (e % 2) * PACK * C : (e % 2 + 1) * PACK * C].rearrange("p (n t) -> p n t", t=4)
+            h0 = 0 if last else (e % 2) * PACK * C
+            half = hb[:, h0 : h0 + PACK * C].rearrange("p (n t) -> p n t", t=4)
             for b in range(banks):
                 part = half[:, :, b * t_a_bank : (b + 1) * t_a_bank]
-                if b == 1:
-                    nc.vector.tensor_scalar_max(out=part, in0=phs[b][:].rearrange("p t n -> p n t"), scalar1=0.0)
-                else:
-                    nc.scalar.activation(out=part, in_=phs[b][:].rearrange("p t n -> p n t"), func=RELU)
-            if e >= E - 2:
-                one_e = slice(e * C, (e + 1) * C)
-                nc.vector.quantize_mx(
-                    out=h_words[:, one_e].bitcast(FP8X4),
-                    scales=h_bytes[:, one_e],
-                    in_=hb[:, (e % 2) * PACK * C : (e % 2 + 1) * PACK * C],
-                )
+                nc.scalar.activation(out=part, in_=phs[b][:].rearrange("p t n -> p n t"), func=RELU)
+            if last:
+                quantise_h(e, hb, h_scales[e])
+            elif e == E - 2:
+                hb_before = hb
             elif e % 2 == 1:
                 pair = slice((e - 1) * C, (e + 1) * C)
                 nc.vector.quantize_mx(out=h_words[:, pair].bitcast(FP8X4), scales=h_bytes[:, pair], in_=hb[:])
@@ -257,16 +277,26 @@ def tile_routed_moe_kernel(tc, xT, w1, w2, gate, offs, pos1, pos2, out):
                     for i in range(W2_EARLY):
                         quantise_w2(i)
                 if e < early_experts:
-                    layer2(e - 1, 2, False)
+                    layer2(e - 1, 2)
 
         for i in range(W2_EARLY, len(W2_PIECES)):
             quantise_w2(i)
-            layer2(W2_PIECES[i][0], W2_PIECES[i][1], i == len(W2_PIECES) - 1)
+        for e0, g in LATE_LAYER2:
+            layer2(e0, g)
 
         first = keep.tile([P, T], F32, name="first")
         second = keep.tile([P, T], F32, name="second")
         total = keep.tile([P, T], F32, name="total")
         nc.vector.tensor_tensor(first[:], y_sb[:].indirect(pos1_t[:]), gate_t[:, 0, :], MULT)
-        nc.vector.tensor_tensor(second[:], y_sb[:].indirect(pos2_t[:]), gate_t[:, 1, :], MULT)
-        nc.vector.tensor_tensor(total[:], first[:], second[:], ADD)
-        nc.sync.dma_start(out=out, in_=total[:])
+        t0 = 0
+        for n in TOKEN_CUTS:
+            cut = slice(t0, t0 + n)
+            picks = pos2_t[:, t0 // 16 : (t0 + n) // 16]
+            nc.vector.tensor_tensor(second[:, cut], y_sb[:].indirect(picks), gate_t[:, 1, cut], MULT)
+            t0 += n
+        t0 = 0
+        for n in TOKEN_CUTS:
+            cut = slice(t0, t0 + n)
+            nc.vector.tensor_tensor(total[:, cut], first[:, cut], second[:, cut], ADD)
+            nc.sync.dma_start(out=out[:, cut], in_=total[:, cut])
+            t0 += n

@@ -80,8 +80,8 @@ def tile_routed_moe_kernel(tc, xT, w1, w2, gate, offs, pos1, pos2, out):
         w2_raw = []
 
         def load_w2(e0, g):
-            if e0 + g == E:
-                r = late.tile([P, g, PACK, N], F32, name="w2_last", tag="late", align_bytes=64)
+            if e0 == E - 2:
+                r = late.tile([P, g, PACK, N], F32, name="w2_late", tag="late", align_bytes=64)
             else:
                 r = ring.tile([P, g, PACK, N], F32, name="w2_raw", tag="raw")
             nc.sync.dma_start(out=r[:], in_=w2[e0 : e0 + g].rearrange("e (p j) n -> p e j n", j=PACK))
@@ -97,8 +97,8 @@ def tile_routed_moe_kernel(tc, xT, w1, w2, gate, offs, pos1, pos2, out):
                 pieces = []
                 c0 = 0
                 for width in widths:
-                    if e == E - 1 and s == PASSES - 1 and c0 + width == H:
-                        r = late.tile([P, PACK, width], F32, name="w1_last", tag="late_w1", align_bytes=64)
+                    if width < H and c0 == 0:
+                        r = late.tile([P, PACK, width], F32, name="w1_late", tag="late_w1", align_bytes=64)
                     else:
                         r = ring.tile([P, PACK, width], F32, name="w1_raw", tag="raw")
                     nc.sync.dma_start(out=r[:], in_=rows[:, :, c0 : c0 + width])
@@ -150,7 +150,10 @@ def tile_routed_moe_kernel(tc, xT, w1, w2, gate, offs, pos1, pos2, out):
 
         def quantise_w2(i):
             e0, g = W2_PIECES[i]
-            st = stage.tile([P, g * PACK * N], BF16, name="w2_st", tag="w2st", align_bytes=64, bufs=4)
+            if e0 == E - 1:
+                st = late.tile([P, g * PACK * N], BF16, name="w2_st_late", tag="late_w2", align_bytes=64)
+            else:
+                st = stage.tile([P, g * PACK * N], BF16, name="w2_st", tag="w2st", align_bytes=64, bufs=3)
             dst = st[:].rearrange("p (e n j) -> p e n j", e=g, j=PACK)
             src = w2_raw[i][:].rearrange("p e j n -> p e n j")
             if i < W2_EARLY:
@@ -160,7 +163,7 @@ def tile_routed_moe_kernel(tc, xT, w1, w2, gate, offs, pos1, pos2, out):
                 v_e = g // 2
                 nc.vector.tensor_copy(out=dst[:, 0:v_e], in_=src[:, 0:v_e])
                 nc.scalar.copy(out=dst[:, v_e:g], in_=src[:, v_e:g])
-            elif i % 2 == 0:
+            elif e0 == E - 1:
                 nc.vector.tensor_copy(out=dst, in_=src)
             else:
                 nc.scalar.copy(out=dst, in_=src)
@@ -195,27 +198,32 @@ def tile_routed_moe_kernel(tc, xT, w1, w2, gate, offs, pos1, pos2, out):
         for e in range(E):
             last = e == E - 1
             if last:
-                st_of = [
-                    stage.tile([P, PACK * H], BF16, name="w1_st_last", tag="st", align_bytes=64),
-                    late.tile([P, PACK * H], BF16, name="w1_st_late", tag="late_st", align_bytes=64),
-                ]
+                st_halves = stage.tile([P, PACK * H], BF16, name="w1_st_last", tag="st", align_bytes=64)
+                st_late = late.tile([P, PACK * H], BF16, name="w1_st_late", tag="late_st", align_bytes=64)
+                st_of = [st_halves, st_late]
             else:
                 st = stage.tile([P, PASSES * PACK * H], BF16, name="w1_st", tag="st", align_bytes=64)
                 st_of = [st[:, s * PACK * H : (s + 1) * PACK * H] for s in range(PASSES)]
             wc = wq.tile([P, PASSES * H], U32, name="w1_words", tag="wc", align_bytes=64)
-            if last:
-                ws = late.tile([P, PASSES * H], U8, name="w1_bytes_last", tag="late_w1", align_bytes=64)
-            else:
-                ws = wq.tile([P, PASSES * H], U8, name="w1_bytes", tag="ws", align_bytes=64)
+            ws = wq.tile([P, PASSES * H], U8, name="w1_bytes", tag="ws", align_bytes=64)
             for s in range(PASSES):
                 pieces = w1_raw[e * PASSES + s]
+                if last and s == 0:
+                    src = pieces[0][0][:].rearrange("p j (m t) -> p m j t", t=4)
+                    half_cols = PACK * H // 2
+                    dst_s = st_halves[:, 0:half_cols].rearrange("p (t m j) -> p m j t", t=2, j=PACK)
+                    dst_v = st_halves[:, half_cols : 2 * half_cols].rearrange("p (t m j) -> p m j t", t=2, j=PACK)
+                    nc.scalar.copy(out=dst_s, in_=src[:, :, :, 0:2])
+                    nc.vector.tensor_copy(out=dst_v, in_=src[:, :, :, 2:4])
+                    nc.vector.quantize_mx(out=wc[:, 0:H].bitcast(FP8X4), scales=ws[:, 0:H], in_=st_halves[:, 0 : PACK * H])
+                    continue
                 whole = st_of[s][:, 0 : PACK * H].rearrange("p (t m j) -> p m j t", t=4, j=PACK)
-                for r, m0, blocks in pieces:
+                for i, (r, m0, blocks) in enumerate(pieces):
                     shared_copy(
                         nc,
                         whole[:, m0 : m0 + blocks],
                         r[:].rearrange("p j (m t) -> p m j t", t=4),
-                        blocks if s == 1 else 0,
+                        blocks if s == 1 and not (last and i == 0) else 0,
                     )
                 if last:
                     nc.vector.quantize_mx(
@@ -259,6 +267,8 @@ def tile_routed_moe_kernel(tc, xT, w1, w2, gate, offs, pos1, pos2, out):
                         pass_of(t, s)
             if last:
                 hb = late.tile([P, PACK * C], BF16, name="hb_last", tag="late", align_bytes=64)
+            elif e == E - 2:
+                hb = late.tile([P, PACK * C], BF16, name="hb_before", tag="late_w1", align_bytes=64)
             elif e % 2 == 0:
                 hb = hst.tile([P, 2 * PACK * C], BF16, name="hb", tag="hb", align_bytes=64)
             h0 = 0 if last else (e % 2) * PACK * C
@@ -267,7 +277,7 @@ def tile_routed_moe_kernel(tc, xT, w1, w2, gate, offs, pos1, pos2, out):
                 part = half[:, :, b * t_a_bank : (b + 1) * t_a_bank]
                 nc.scalar.activation(out=part, in_=phs[b][:].rearrange("p t n -> p n t"), func=RELU)
             if last:
-                quantise_h(e, hb, h_scales[e])
+                hb_last = hb
             elif e == E - 2:
                 hb_before = hb
             elif e % 2 == 1:
@@ -281,6 +291,8 @@ def tile_routed_moe_kernel(tc, xT, w1, w2, gate, offs, pos1, pos2, out):
 
         for i in range(W2_EARLY, len(W2_PIECES)):
             quantise_w2(i)
+        last_scales = late.tile([P, C], U8, name="h_bytes_last", tag="late_w2", align_bytes=64)
+        quantise_h(E - 1, hb_last, last_scales[:])
         for e0, g in LATE_LAYER2:
             layer2(e0, g)
 

@@ -23,7 +23,7 @@ FLOPS = 2 * SLOTS * (K * H + H * N)
 
 SLICES = ((0, 384), (384, 384), (768, 256))
 EXPERTS_A_SLICE = 3
-LAST_WIDTHS = (256, 128, 128)
+HALF = H // 2
 RING = 13
 V_BLOCKS = (0, 128)
 G_BLOCKS = (0, 0)
@@ -93,22 +93,16 @@ def tile_routed_moe_kernel(tc, xT, w1, w2, gate, offs, pos1, pos2, out):
         for e in range(E):
             for s in range(PASSES):
                 rows = w1[e, s * K_PASS : (s + 1) * K_PASS, :].rearrange("(p j) c -> p j c", j=PACK)
-                widths = LAST_WIDTHS if (e == E - 1 and s == PASSES - 1) else (H,)
-                pieces = []
-                c0 = 0
-                for width in widths:
-                    if width < H and c0 == 0:
-                        r = late.tile([P, PACK, width], F32, name="w1_late", tag="late_w1", align_bytes=64)
-                    else:
-                        r = ring.tile([P, PACK, width], F32, name="w1_raw", tag="raw")
-                    nc.sync.dma_start(out=r[:], in_=rows[:, :, c0 : c0 + width])
-                    pieces.append((r, c0 // 4, width // 4))
-                    c0 += width
-                w1_raw.append(pieces)
+                r = ring.tile([P, PACK, H], F32, name="w1_raw", tag="raw")
+                nc.sync.dma_start(out=r[:], in_=rows)
+                w1_raw.append(r)
         for e0, g in W2_PIECES[W2_EARLY:]:
             load_w2(e0, g)
-        gate_t = ring.tile([P, 2, T], F32, name="gate_t", tag="raw")
-        nc.sync.dma_start(out=gate_t[:], in_=gate.rearrange("r n t -> n r t"))
+        gates = []
+        for r in range(2):
+            gate_t = ring.tile([P, T], F32, name="gate_t", tag="raw")
+            nc.sync.dma_start(out=gate_t[:], in_=gate[r])
+            gates.append(gate_t)
 
         x_words = []
         for s in range(PASSES):
@@ -198,39 +192,33 @@ def tile_routed_moe_kernel(tc, xT, w1, w2, gate, offs, pos1, pos2, out):
         for e in range(E):
             last = e == E - 1
             if last:
-                st_halves = stage.tile([P, PACK * H], BF16, name="w1_st_last", tag="st", align_bytes=64)
+                st_first = stage.tile([P, PACK * H], BF16, name="w1_st_last", tag="st", align_bytes=64)
                 st_late = late.tile([P, PACK * H], BF16, name="w1_st_late", tag="late_st", align_bytes=64)
-                st_of = [st_halves, st_late]
+                st_of = [st_first, st_late]
             else:
                 st = stage.tile([P, PASSES * PACK * H], BF16, name="w1_st", tag="st", align_bytes=64)
-                st_of = [st[:, s * PACK * H : (s + 1) * PACK * H] for s in range(PASSES)]
             wc = wq.tile([P, PASSES * H], U32, name="w1_words", tag="wc", align_bytes=64)
             ws = wq.tile([P, PASSES * H], U8, name="w1_bytes", tag="ws", align_bytes=64)
             for s in range(PASSES):
-                pieces = w1_raw[e * PASSES + s]
-                if last and s == 0:
-                    src = pieces[0][0][:].rearrange("p j (m t) -> p m j t", t=4)
-                    half_cols = PACK * H // 2
-                    dst_s = st_halves[:, 0:half_cols].rearrange("p (t m j) -> p m j t", t=2, j=PACK)
-                    dst_v = st_halves[:, half_cols : 2 * half_cols].rearrange("p (t m j) -> p m j t", t=2, j=PACK)
-                    nc.scalar.copy(out=dst_s, in_=src[:, :, :, 0:2])
-                    nc.vector.tensor_copy(out=dst_v, in_=src[:, :, :, 2:4])
-                    nc.vector.quantize_mx(out=wc[:, 0:H].bitcast(FP8X4), scales=ws[:, 0:H], in_=st_halves[:, 0 : PACK * H])
-                    continue
-                whole = st_of[s][:, 0 : PACK * H].rearrange("p (t m j) -> p m j t", t=4, j=PACK)
-                for i, (r, m0, blocks) in enumerate(pieces):
-                    shared_copy(
-                        nc,
-                        whole[:, m0 : m0 + blocks],
-                        r[:].rearrange("p j (m t) -> p m j t", t=4),
-                        blocks if s == 1 and not (last and i == 0) else 0,
-                    )
+                src = w1_raw[e * PASSES + s][:].rearrange("p j (m t) -> p m j t", t=4)
                 if last:
-                    nc.vector.quantize_mx(
-                        out=wc[:, s * H : (s + 1) * H].bitcast(FP8X4),
-                        scales=ws[:, s * H : (s + 1) * H],
-                        in_=st_of[s][:, 0 : PACK * H],
-                    )
+                    for g in range(2):
+                        dst = st_of[s][:, g * HALF * PACK : (g + 1) * HALF * PACK]
+                        dst = dst.rearrange("p (t m j) -> p m j t", t=2, j=PACK)
+                        if g == 0:
+                            nc.scalar.copy(out=dst, in_=src[:, :, :, 0:2])
+                        else:
+                            nc.vector.tensor_copy(out=dst, in_=src[:, :, :, 2:4])
+                    for c0, n in ((0, H),) if s == 0 else ((HALF, HALF), (0, HALF)):
+                        cols = slice(s * H + c0, s * H + c0 + n)
+                        nc.vector.quantize_mx(
+                            out=wc[:, cols].bitcast(FP8X4),
+                            scales=ws[:, cols],
+                            in_=st_of[s][:, PACK * c0 : PACK * (c0 + n)],
+                        )
+                else:
+                    dst = st[:, s * PACK * H : (s + 1) * PACK * H].rearrange("p (t m j) -> p m j t", t=4, j=PACK)
+                    shared_copy(nc, dst, src, P if s == 1 else 0)
             if last:
                 before_scales = late.tile([P, C], U8, name="h_bytes_before", tag="late_st", align_bytes=64)
                 quantise_h(E - 2, hb_before, before_scales[:])
@@ -258,22 +246,21 @@ def tile_routed_moe_kernel(tc, xT, w1, w2, gate, offs, pos1, pos2, out):
                     stop=(s == PASSES - 1),
                 )
 
-            for b in range(banks):
+            order = range(banks - 1, -1, -1)
+            for b in order:
                 pass_of(b * t_a_bank, 0)
-            for b in range(banks):
+            for b in order:
                 pass_of(b * t_a_bank, 1)
                 for t in range(b * t_a_bank + 1, (b + 1) * t_a_bank):
                     for s in range(PASSES):
                         pass_of(t, s)
             if last:
                 hb = late.tile([P, PACK * C], BF16, name="hb_last", tag="late", align_bytes=64)
-            elif e == E - 2:
-                hb = late.tile([P, PACK * C], BF16, name="hb_before", tag="late_w1", align_bytes=64)
             elif e % 2 == 0:
                 hb = hst.tile([P, 2 * PACK * C], BF16, name="hb", tag="hb", align_bytes=64)
             h0 = 0 if last else (e % 2) * PACK * C
             half = hb[:, h0 : h0 + PACK * C].rearrange("p (n t) -> p n t", t=4)
-            for b in range(banks):
+            for b in order:
                 part = half[:, :, b * t_a_bank : (b + 1) * t_a_bank]
                 nc.scalar.activation(out=part, in_=phs[b][:].rearrange("p t n -> p n t"), func=RELU)
             if last:
@@ -299,12 +286,12 @@ def tile_routed_moe_kernel(tc, xT, w1, w2, gate, offs, pos1, pos2, out):
         first = keep.tile([P, T], F32, name="first")
         second = keep.tile([P, T], F32, name="second")
         total = keep.tile([P, T], F32, name="total")
-        nc.vector.tensor_tensor(first[:], y_sb[:].indirect(pos1_t[:]), gate_t[:, 0, :], MULT)
+        nc.vector.tensor_tensor(first[:], y_sb[:].indirect(pos1_t[:]), gates[0][:], MULT)
         t0 = 0
         for n in TOKEN_CUTS:
             cut = slice(t0, t0 + n)
             picks = pos2_t[:, t0 // 16 : (t0 + n) // 16]
-            nc.vector.tensor_tensor(second[:, cut], y_sb[:].indirect(picks), gate_t[:, 1, cut], MULT)
+            nc.vector.tensor_tensor(second[:, cut], y_sb[:].indirect(picks), gates[1][:, cut], MULT)
             t0 += n
         t0 = 0
         for n in TOKEN_CUTS:

@@ -24,7 +24,7 @@ FLOPS = 2 * SLOTS * (K * H + H * N)
 SLICES = ((0, 384), (384, 384), (768, 256))
 EXPERTS_A_SLICE = 3
 HALF = H // 2
-RING = 13
+RING = 12
 V_BLOCKS = (0, 128)
 G_BLOCKS = (0, 0)
 LAST_V_BLOCKS = (0, 128)
@@ -73,10 +73,6 @@ def tile_routed_moe_kernel(tc, xT, w1, w2, gate, offs, pos1, pos2, out):
             r = ring.tile([P, PACK, T], F32, name="x_raw", tag="raw")
             nc.sync.dma_start(out=r[:], in_=xT[s * K_PASS : (s + 1) * K_PASS, :].rearrange("(p j) t -> p j t", j=PACK))
             x_raw.append(r)
-        pos1_t = lists.tile([P, T // 16], U16, name="pos1_t")
-        nc.sync.dma_start(pos1_t[:], pos1)
-        pos2_t = lists.tile([P, T // 16], U16, name="pos2_t")
-        nc.sync.dma_start(pos2_t[:], pos2)
         w2_raw = []
 
         def load_w2(e0, g):
@@ -84,7 +80,12 @@ def tile_routed_moe_kernel(tc, xT, w1, w2, gate, offs, pos1, pos2, out):
                 r = late.tile([P, g, PACK, N], F32, name="w2_late", tag="late", align_bytes=64)
             else:
                 r = ring.tile([P, g, PACK, N], F32, name="w2_raw", tag="raw")
-            nc.sync.dma_start(out=r[:], in_=w2[e0 : e0 + g].rearrange("e (p j) n -> p e j n", j=PACK))
+            if e0 == E - 1:
+                pairs = w2[e0].rearrange("(g h r v) n -> h g r (v n)", h=2, r=2, v=2)
+                for h in range(2):
+                    nc.sync.dma_start(out=r[:, 0, 2 * h : 2 * h + 2, :].rearrange("p v n -> p (v n)"), in_=pairs[h])
+            else:
+                nc.sync.dma_start(out=r[:], in_=w2[e0 : e0 + g].rearrange("e (p j) n -> p e j n", j=PACK))
             w2_raw.append(r)
 
         for e0, g in W2_PIECES[:W2_EARLY]:
@@ -93,11 +94,18 @@ def tile_routed_moe_kernel(tc, xT, w1, w2, gate, offs, pos1, pos2, out):
         for e in range(E):
             for s in range(PASSES):
                 rows = w1[e, s * K_PASS : (s + 1) * K_PASS, :].rearrange("(p j) c -> p j c", j=PACK)
-                r = ring.tile([P, PACK, H], F32, name="w1_raw", tag="raw")
+                if e == E - 1 and s == PASSES - 1:
+                    r = late.tile([P, PACK, H], F32, name="w1_late", tag="late_w1", align_bytes=64)
+                else:
+                    r = ring.tile([P, PACK, H], F32, name="w1_raw", tag="raw")
                 nc.sync.dma_start(out=r[:], in_=rows)
                 w1_raw.append(r)
         for e0, g in W2_PIECES[W2_EARLY:]:
             load_w2(e0, g)
+        pos1_t = lists.tile([P, T // 16], U16, name="pos1_t")
+        nc.sync.dma_start(pos1_t[:], pos1)
+        pos2_t = lists.tile([P, T // 16], U16, name="pos2_t")
+        nc.sync.dma_start(pos2_t[:], pos2)
         gates = []
         for r in range(2):
             gate_t = ring.tile([P, T], F32, name="gate_t", tag="raw")
@@ -200,15 +208,16 @@ def tile_routed_moe_kernel(tc, xT, w1, w2, gate, offs, pos1, pos2, out):
             wc = wq.tile([P, PASSES * H], U32, name="w1_words", tag="wc", align_bytes=64)
             ws = wq.tile([P, PASSES * H], U8, name="w1_bytes", tag="ws", align_bytes=64)
             for s in range(PASSES):
-                src = w1_raw[e * PASSES + s][:].rearrange("p j (m t) -> p m j t", t=4)
+                src = w1_raw[e * PASSES + s]
                 if last:
-                    for g in range(2):
-                        dst = st_of[s][:, g * HALF * PACK : (g + 1) * HALF * PACK]
-                        dst = dst.rearrange("p (t m j) -> p m j t", t=2, j=PACK)
-                        if g == 0:
-                            nc.scalar.copy(out=dst, in_=src[:, :, :, 0:2])
+                    src = src[:].rearrange("p j (g h r v) -> p h g j r v", h=2, r=2, v=2)
+                    for h in range(2):
+                        dst = st_of[s][:, h * HALF * PACK : (h + 1) * HALF * PACK]
+                        dst = dst.rearrange("p (v g r j) -> p g j r v", v=2, r=2, j=PACK)
+                        if h == 0:
+                            nc.scalar.copy(out=dst, in_=src[:, h])
                         else:
-                            nc.vector.tensor_copy(out=dst, in_=src[:, :, :, 2:4])
+                            nc.vector.tensor_copy(out=dst, in_=src[:, h])
                     for c0, n in ((0, H),) if s == 0 else ((HALF, HALF), (0, HALF)):
                         cols = slice(s * H + c0, s * H + c0 + n)
                         nc.vector.quantize_mx(
@@ -218,7 +227,7 @@ def tile_routed_moe_kernel(tc, xT, w1, w2, gate, offs, pos1, pos2, out):
                         )
                 else:
                     dst = st[:, s * PACK * H : (s + 1) * PACK * H].rearrange("p (t m j) -> p m j t", t=4, j=PACK)
-                    shared_copy(nc, dst, src, P if s == 1 else 0)
+                    shared_copy(nc, dst, src[:].rearrange("p j (m t) -> p m j t", t=4), P if s == 1 else 0)
             if last:
                 before_scales = late.tile([P, C], U8, name="h_bytes_before", tag="late_st", align_bytes=64)
                 quantise_h(E - 2, hb_before, before_scales[:])
@@ -256,6 +265,8 @@ def tile_routed_moe_kernel(tc, xT, w1, w2, gate, offs, pos1, pos2, out):
                         pass_of(t, s)
             if last:
                 hb = late.tile([P, PACK * C], BF16, name="hb_last", tag="late", align_bytes=64)
+            elif e == E - 2:
+                hb = late.tile([P, PACK * C], BF16, name="hb_before", tag="late_w1", align_bytes=64)
             elif e % 2 == 0:
                 hb = hst.tile([P, 2 * PACK * C], BF16, name="hb", tag="hb", align_bytes=64)
             h0 = 0 if last else (e % 2) * PACK * C

@@ -162,9 +162,7 @@ def tile_routed_moe_kernel(tc, xT, w1, w2, gate, offs, pos1, pos2, out):
                 for a in range(0, g, 2):
                     nc.scalar.copy(out=dst[:, a : a + 2], in_=src[:, a : a + 2])
             elif g > 1:
-                v_e = g // 2
-                nc.vector.tensor_copy(out=dst[:, 0:v_e], in_=src[:, 0:v_e])
-                nc.scalar.copy(out=dst[:, v_e:g], in_=src[:, v_e:g])
+                nc.vector.tensor_copy(out=dst, in_=src)
             elif e0 == E - 1:
                 nc.vector.tensor_copy(out=dst, in_=src)
             else:

@@ -63,7 +63,7 @@ def tile_routed_moe_kernel(tc, xT, w1, w2, gate, offs, pos1, pos2, out):
         gat = ctx.enter_context(tc.tile_pool(name="gat", bufs=2))
         hst = ctx.enter_context(tc.tile_pool(name="hst", bufs=2))
         late = ctx.enter_context(tc.tile_pool(name="late", bufs=1))
-        psum_h = ctx.enter_context(tc.psum_pool(name="psum_h", bufs=2))
+        psum_h = ctx.enter_context(tc.psum_pool(name="psum_h", bufs=3))
         psum_y = ctx.enter_context(tc.psum_pool(name="psum_y", bufs=1))
 
         offs_t = lists.tile([P, SLOTS // 16], U16, name="offs_t")

from contextlib import ExitStack

import concourse.mybir as mybir

F32 = mybir.dt.float32
BF16 = mybir.dt.bfloat16
U32 = mybir.dt.uint32
U16 = mybir.dt.uint16
U8 = mybir.dt.uint8
FP8X4 = mybir.dt.float8_e4m3fn_x4
MULT = mybir.AluOpType.mult
ADD = mybir.AluOpType.add
MAX = mybir.AluOpType.max
RELU = mybir.ActivationFunctionType.Relu

P = 128
K, T, E, C, H, N = 1024, 512, 8, 128, 512, 128
PACK = 4
K_PASS = P * PACK
PASSES = K // K_PASS
SLOTS = E * C
FLOPS = 2 * SLOTS * (K * H + H * N)

SLICES = ((0, 384), (384, 384), (768, 256))
EXPERTS_A_SLICE = 3
HALF = H // 2
RING = 12
V_BLOCKS = (0, 128)
G_BLOCKS = (0, 0)
LAST_V_BLOCKS = (0, 128)
X_V_BLOCKS = 80
W2_PIECES = ((0, 4), (4, 2), (6, 1), (7, 1))
LATE_LAYER2 = ((4, 3), (7, 1))
W2_EARLY = 1
TOKEN_CUTS = (320, 192)


def shared_copy(nc, dst, src, v_count, g_count=0):
    total = dst.shape[1]
    if v_count > 0:
        nc.vector.tensor_copy(out=dst[:, 0:v_count], in_=src[:, 0:v_count])
    if g_count > 0:
        nc.gpsimd.tensor_scalar(
            out=dst[:, v_count : v_count + g_count].rearrange("p m j t -> p t m j"),
            in0=src[:, v_count : v_count + g_count].rearrange("p m j t -> p t m j"),
            scalar1=1.0,
            scalar2=0.0,
            op0=MULT,
            op1=ADD,
        )
    if v_count + g_count < total:
        nc.scalar.copy(out=dst[:, v_count + g_count : total], in_=src[:, v_count + g_count : total])


def tile_routed_moe_kernel(tc, xT, w1, w2, gate, offs, pos1, pos2, out):
    nc = tc.nc
    with ExitStack() as ctx:
        lists = ctx.enter_context(tc.tile_pool(name="lists", bufs=1))
        keep = ctx.enter_context(tc.tile_pool(name="keep", bufs=1))
        ring = ctx.enter_context(tc.tile_pool(name="ring", bufs=RING))
        stage = ctx.enter_context(tc.tile_pool(name="stage", bufs=5))
        wq = ctx.enter_context(tc.tile_pool(name="wq", bufs=4))
        gat = ctx.enter_context(tc.tile_pool(name="gat", bufs=2))
        hst = ctx.enter_context(tc.tile_pool(name="hst", bufs=2))
        late = ctx.enter_context(tc.tile_pool(name="late", bufs=1))
        psum_h = ctx.enter_context(tc.psum_pool(name="psum_h", bufs=3))
        psum_y = ctx.enter_context(tc.psum_pool(name="psum_y", bufs=1))

        offs_t = lists.tile([P, SLOTS // 16], U16, name="offs_t")
        nc.sync.dma_start(offs_t[:], offs)
        x_raw = []
        for s in range(PASSES):
            r = ring.tile([P, PACK, T], F32, name="x_raw", tag="raw")
            nc.sync.dma_start(out=r[:], in_=xT[s * K_PASS : (s + 1) * K_PASS, :].rearrange("(p j) t -> p j t", j=PACK))
            x_raw.append(r)
        w2_raw = []

        def load_w2(e0, g):
            if e0 == E - 2:
                r = late.tile([P, g, PACK, N], F32, name="w2_late", tag="late", align_bytes=64)
            else:
                r = ring.tile([P, g, PACK, N], F32, name="w2_raw", tag="raw")
            if e0 == E - 1:
                pairs = w2[e0].rearrange("(g h r v) n -> h g r (v n)", h=2, r=2, v=2)
                for h in range(2):
                    nc.sync.dma_start(out=r[:, 0, 2 * h : 2 * h + 2, :].rearrange("p v n -> p (v n)"), in_=pairs[h])
            else:
                nc.sync.dma_start(out=r[:], in_=w2[e0 : e0 + g].rearrange("e (p j) n -> p e j n", j=PACK))
            w2_raw.append(r)

        for e0, g in W2_PIECES[:W2_EARLY]:
            load_w2(e0, g)
        w1_raw = []
        for e in range(E):
            for s in range(PASSES):
                rows = w1[e, s * K_PASS : (s + 1) * K_PASS, :].rearrange("(p j) c -> p j c", j=PACK)
                if e == E - 1 and s == PASSES - 1:
                    r = late.tile([P, PACK, H], F32, name="w1_late", tag="late_w1", align_bytes=64)
                else:
                    r = ring.tile([P, PACK, H], F32, name="w1_raw", tag="raw")
                nc.sync.dma_start(out=r[:], in_=rows)
                w1_raw.append(r)
        for e0, g in W2_PIECES[W2_EARLY:]:
            load_w2(e0, g)
        pos1_t = lists.tile([P, T // 16], U16, name="pos1_t")
        nc.sync.dma_start(pos1_t[:], pos1)
        pos2_t = lists.tile([P, T // 16], U16, name="pos2_t")
        nc.sync.dma_start(pos2_t[:], pos2)
        gates = []
        for r in range(2):
            gate_t = ring.tile([P, T], F32, name="gate_t", tag="raw")
            nc.sync.dma_start(out=gate_t[:], in_=gate[r])
            gates.append(gate_t)

        x_words = []
        for s in range(PASSES):
            xw = keep.tile([P, T], U32, name="x_words%d" % s, align_bytes=64)
            x_words.append(xw)
        x_bytes = keep.tile([P, T], U8, name="x_bytes", align_bytes=64)
        nc.gpsimd.memset(x_bytes[:], 0)
        x_planes = [x_bytes[PACK * s : P, :] for s in range(PASSES)]

        x_st = []
        for s in range(PASSES):
            st = stage.tile([P, PACK * T], BF16, name="x_st", tag="xst", align_bytes=64, bufs=2)
            shared_copy(
                nc,
                st[:].rearrange("p (c i j) -> p c j i", i=4, j=PACK),
                x_raw[s][:].rearrange("p j (c i) -> p c j i", i=4),
                X_V_BLOCKS if s == 0 else 0,
            )
            x_st.append(st)
        for s in range(PASSES):
            nc.vector.quantize_mx(out=x_words[s][:].bitcast(FP8X4), scales=x_planes[s], in_=x_st[s][:])

        def gather(q):
            j0, n = SLICES[q]
            picks = offs_t[:, j0 // 16 : (j0 + n) // 16]
            gw = gat.tile([P, PASSES, n], U32, name="g_words", tag="gw", align_bytes=64)
            for s in range(PASSES):
                nc.vector.tensor_copy(out=gw[:, s, :], in_=x_words[s][:].indirect(picks))
            gb = gat.tile([P, n], U8, name="g_bytes", tag="gb", align_bytes=64)
            nc.vector.tensor_copy(out=gb[:], in_=x_bytes[:].indirect(picks))
            return gw, gb

        h_words = keep.tile([P, SLOTS], U32, name="h_words", align_bytes=64)
        h_bytes = keep.tile([P, SLOTS], U8, name="h_bytes", align_bytes=64)
        w2_words = keep.tile([P, E * N], U32, name="w2_words", align_bytes=64)
        w2_bytes = keep.tile([P, E * N], U8, name="w2_bytes", align_bytes=64)
        h_scales = [h_bytes[:, e * C : (e + 1) * C] for e in range(E)]
        y_sb = keep.tile([P, SLOTS], F32, name="y_sb")

        def quantise_w2(i):
            e0, g = W2_PIECES[i]
            if e0 == E - 1:
                st = late.tile([P, g * PACK * N], BF16, name="w2_st_late", tag="late_w2", align_bytes=64)
            else:
                st = stage.tile([P, g * PACK * N], BF16, name="w2_st", tag="w2st", align_bytes=64, bufs=3)
            dst = st[:].rearrange("p (e n j) -> p e n j", e=g, j=PACK)
            src = w2_raw[i][:].rearrange("p e j n -> p e n j")
            if i < W2_EARLY:
                for a in range(0, g, 2):
                    nc.scalar.copy(out=dst[:, a : a + 2], in_=src[:, a : a + 2])
            elif g > 1:
                nc.vector.tensor_copy(out=dst, in_=src)
            elif e0 == E - 1:
                nc.vector.tensor_copy(out=dst, in_=src)
            else:
                nc.scalar.copy(out=dst, in_=src)
            cols = slice(e0 * N, (e0 + g) * N)
            nc.vector.quantize_mx(out=w2_words[:, cols].bitcast(FP8X4), scales=w2_bytes[:, cols], in_=st[:])

        def layer2(e0, g):
            if e0 == LATE_LAYER2[0][0]:
                py = psum_h.tile([P, g, C], F32, name="py_late", tag="ph")
            else:
                py = psum_y.tile([P, g, C], F32, name="py%d" % e0)
            for a in range(g):
                one = slice((e0 + a) * C, (e0 + a + 1) * C)
                nc.tensor.matmul_mx(
                    out=py[:, a, :],
                    lhsT=w2_words[:, one].bitcast(FP8X4),
                    lhsT_scale=w2_bytes[:, one],
                    rhs=h_words[:, one].bitcast(FP8X4),
                    rhs_scale=h_scales[e0 + a],
                    start=True,
                    stop=True,
                )
            y_cols = y_sb[:, e0 * C : (e0 + g) * C]
            nc.scalar.copy(out=y_cols, in_=py[:].rearrange("p a c -> p (a c)"))

        def quantise_h(e, hb, scales):
            one = slice(e * C, (e + 1) * C)
            nc.vector.quantize_mx(out=h_words[:, one].bitcast(FP8X4), scales=scales, in_=hb[:, 0 : PACK * C])
            h_scales[e] = scales

        early_experts = sum(g for e0, g in W2_PIECES[:W2_EARLY])
        for e in range(E):
            last = e == E - 1
            if last:
                st_first = stage.tile([P, PACK * H], BF16, name="w1_st_last", tag="st", align_bytes=64)
                st_late = late.tile([P, PACK * H], BF16, name="w1_st_late", tag="late_st", align_bytes=64)
                st_of = [st_first, st_late]
            else:
                st = stage.tile([P, PASSES * PACK * H], BF16, name="w1_st", tag="st", align_bytes=64)
            wc = wq.tile([P, PASSES * H], U32, name="w1_words", tag="wc", align_bytes=64)
            ws = wq.tile([P, PASSES * H], U8, name="w1_bytes", tag="ws", align_bytes=64)
            for s in range(PASSES):
                src = w1_raw[e * PASSES + s]
                if last:
                    src = src[:].rearrange("p j (g h r v) -> p h g j r v", h=2, r=2, v=2)
                    for h in range(2):
                        dst = st_of[s][:, h * HALF * PACK : (h + 1) * HALF * PACK]
                        dst = dst.rearrange("p (v g r j) -> p g j r v", v=2, r=2, j=PACK)
                        if h == 0:
                            nc.scalar.copy(out=dst, in_=src[:, h])
                        else:
                            nc.vector.tensor_copy(out=dst, in_=src[:, h])
                    for c0, n in ((0, H),) if s == 0 else ((HALF, HALF), (0, HALF)):
                        cols = slice(s * H + c0, s * H + c0 + n)
                        nc.vector.quantize_mx(
                            out=wc[:, cols].bitcast(FP8X4),
                            scales=ws[:, cols],
                            in_=st_of[s][:, PACK * c0 : PACK * (c0 + n)],
                        )
                else:
                    dst = st[:, s * PACK * H : (s + 1) * PACK * H].rearrange("p (t m j) -> p m j t", t=4, j=PACK)
                    shared_copy(nc, dst, src[:].rearrange("p j (m t) -> p m j t", t=4), P if s == 1 else 0)
            if last:
                before_scales = late.tile([P, C], U8, name="h_bytes_before", tag="late_st", align_bytes=64)
                quantise_h(E - 2, hb_before, before_scales[:])
            else:
                nc.vector.quantize_mx(out=wc[:].bitcast(FP8X4), scales=ws[:], in_=st[:])
            if e % EXPERTS_A_SLICE == 0:
                g_words, g_bytes = gather(e // EXPERTS_A_SLICE)
            mine = slice((e % EXPERTS_A_SLICE) * C, (e % EXPERTS_A_SLICE + 1) * C)
            banks = 2 if last else 1
            t_a_bank = 4 // banks
            phs = []
            for b in range(banks):
                ph = psum_h.tile([P, t_a_bank, C], F32, name="ph", tag="ph")
                phs.append(ph)

            def pass_of(t, s):
                w_cols = slice(s * H + t * P, s * H + (t + 1) * P)
                nc.tensor.matmul_mx(
                    out=phs[t // t_a_bank][:, t % t_a_bank, :],
                    lhsT=wc[:, w_cols].bitcast(FP8X4),
                    lhsT_scale=ws[:, w_cols],
                    rhs=g_words[:, s, mine].bitcast(FP8X4),
                    rhs_scale=g_bytes[PACK * s : P, mine],
                    start=(s == 0),
                    stop=(s == PASSES - 1),
                )

            order = range(banks - 1, -1, -1)
            for b in order:
                pass_of(b * t_a_bank, 0)
            for b in order:
                pass_of(b * t_a_bank, 1)
                for t in range(b * t_a_bank + 1, (b + 1) * t_a_bank):
                    for s in range(PASSES):
                        pass_of(t, s)
            if last:
                hb = late.tile([P, PACK * C], BF16, name="hb_last", tag="late", align_bytes=64)
            elif e == E - 2:
                hb = late.tile([P, PACK * C], BF16, name="hb_before", tag="late_w1", align_bytes=64)
            elif e % 2 == 0:
                hb = hst.tile([P, 2 * PACK * C], BF16, name="hb", tag="hb", align_bytes=64)
            h0 = 0 if last else (e % 2) * PACK * C
            half = hb[:, h0 : h0 + PACK * C].rearrange("p (n t) -> p n t", t=4)
            for b in order:
                part = half[:, :, b * t_a_bank : (b + 1) * t_a_bank]
                nc.scalar.activation(out=part, in_=phs[b][:].rearrange("p t n -> p n t"), func=RELU)
            if last:
                hb_last = hb
            elif e == E - 2:
                hb_before = hb
            elif e % 2 == 1:
                pair = slice((e - 1) * C, (e + 1) * C)
                nc.vector.quantize_mx(out=h_words[:, pair].bitcast(FP8X4), scales=h_bytes[:, pair], in_=hb[:])
                if e == 1:
                    for i in range(W2_EARLY):
                        quantise_w2(i)
                if e < early_experts:
                    layer2(e - 1, 2)

        for i in range(W2_EARLY, len(W2_PIECES)):
            quantise_w2(i)
        last_scales = late.tile([P, C], U8, name="h_bytes_last", tag="late_w2", align_bytes=64)
        quantise_h(E - 1, hb_last, last_scales[:])
        for e0, g in LATE_LAYER2:
            layer2(e0, g)

        first = keep.tile([P, T], F32, name="first")
        second = keep.tile([P, T], F32, name="second")
        total = keep.tile([P, T], F32, name="total")
        nc.vector.tensor_tensor(first[:], y_sb[:].indirect(pos1_t[:]), gates[0][:], MULT)
        t0 = 0
        for n in TOKEN_CUTS:
            cut = slice(t0, t0 + n)
            picks = pos2_t[:, t0 // 16 : (t0 + n) // 16]
            nc.vector.tensor_tensor(second[:, cut], y_sb[:].indirect(picks), gates[1][:, cut], MULT)
            t0 += n
        t0 = 0
        for n in TOKEN_CUTS:
            cut = slice(t0, t0 + n)
            nc.vector.tensor_tensor(total[:, cut], first[:, cut], second[:, cut], ADD)
            nc.sync.dma_start(out=out[:, cut], in_=total[:, cut])
            t0 += n
